import numpy as np
CORES = [96,97,98,99,224,225,226,227,352,353,354,355,480,481,482,483]
N = 16
def setup_inputs(rng):
    return {"x": rng.standard_normal((N, 128, 4), dtype=np.float32)}
def reference(x):
    s = x.sum(axis=0, dtype=np.float64).astype(x.dtype)
    s = np.maximum(s, 0)
    return {"y": np.broadcast_to(s, (N,) + s.shape)}

from concourse.bass import DstId, RemoteDMATransfer
from concourse.mybir import AluOpType

SCRATCH = {
    "slots": ("dram", [8, 128, 4], "float32"),
    "land": ("sbuf", [128, 8], "float32"),
    "zero": ("sbuf", [128, 4], "float32"),
    "tmp": ("sbuf", [128, 4], "float32"),
    "out": ("sbuf", [128, 4], "float32"),
}
SEMAPHORES = ["ld", "arr1", "arr2", "sent", "vz", "va", "vm", "st"]


def rank_program(g, core, T, topo):
    rank = T.rank_of(core)
    if rank is None:
        return
    cores = T.cores
    h, j = rank // 4, rank % 4
    slot = rank % 8
    rack0 = rank - slot

    def dst(d):
        rid, pid = topo.addr(d, core)
        return DstId(rid=rid, pnc=pid)

    g.vector.memset(T.zero[:], 0.0).then_inc(T.sem.vz, 1)

    g.sync.dma_start(T.slots[slot], T.x[:]).then_inc(T.sem.ld, 16)
    g.wait_ge(T.sem.ld, 16)

    peers = [cores[rack0 + k] for k in range(8) if k != slot]
    far = [p for p in peers if topo.host(p) != topo.host(core)]
    near = [p for p in peers if topo.host(p) == topo.host(core)]
    transfers = []
    for i, p in enumerate(far + near):
        transfers.append(RemoteDMATransfer(
            dst_ids=[dst(p)], dma_engine_mask=0x3 << (2 * i), remote_sem=T.sem.arr1,
            src=T.slots[slot], dst=T.slots[slot], alu_op=0))
    g.remote_dma_fused(transfers, local_sem=T.sem.sent)
    g.wait_ge(T.sem.arr1, 7 * 2)

    cable = cores[4 * (3 - h) + j]
    neighbour = cores[4 * h + (j + 1) % 4]
    srcs = [T.slots[k] for k in range(8)]
    g.remote_dma_fused([
        RemoteDMATransfer(dst_ids=[dst(cable)], dma_engine_mask=0x00FF, remote_sem=T.sem.arr2,
                          srcs=srcs, dsts=[T.land[:, 4:8]], alu_op=1),
        RemoteDMATransfer(dst_ids=[dst(neighbour)], dma_engine_mask=0xFF00, remote_sem=T.sem.arr2,
                          srcs=srcs, dsts=[T.land[:, 0:4]], alu_op=1),
    ], local_sem=T.sem.sent)

    v = g.vector
    v.wait_ge(T.sem.vz, 1)
    v.wait_ge(T.sem.arr2, 16)
    v.tensor_tensor(T.tmp[:], T.land[:, 0:4], T.land[:, 4:8], AluOpType.add).then_inc(T.sem.va, 1)
    v.wait_ge(T.sem.va, 1)
    v.tensor_tensor(T.out[:], T.tmp[:], T.zero[:], AluOpType.max).then_inc(T.sem.vm, 1)
    g.sync.wait_ge(T.sem.vm, 1)
    g.sync.dma_start(T.y[:], T.out[:]).then_inc(T.sem.st, 16)
    g.sync.wait_ge(T.sem.st, 16)

    g.wait_ge(T.sem.sent, 14 + 16)
